import numpy as np
import ml_dtypes


def mxq(x, axis, fmt="e4m3"):
    dtype, down = {"e4m3": (ml_dtypes.float8_e4m3fn, 7), "e5m2": (ml_dtypes.float8_e5m2, 14)}[fmt]
    v = np.moveaxis(np.asarray(x, np.float32).astype(ml_dtypes.bfloat16).astype(np.float64), axis, -1)
    blocks = v.reshape(v.shape[:-1] + (-1, 32))
    amax = np.abs(blocks).max(-1, keepdims=True)
    byte = np.maximum(np.where(amax > 0, np.frexp(amax)[1] - 1 + 127, 0) - down, 1)
    scale = np.exp2(byte - 127.0)
    codes = (blocks / scale).astype(np.float32).astype(dtype).astype(np.float64)
    return np.moveaxis((codes * scale).reshape(v.shape), -1, axis)


WIDE = False


def mx_kscale(k, group=512):
    if not WIDE:
        return np.ones(k)
    levels = np.array([10, -10, 5, -5, 0])
    if group != 512:
        return np.exp2(np.random.permutation(np.resize(levels, k // group))).repeat(group)
    if k % 512:
        return np.exp2(np.random.permutation(np.resize(levels, k // 32))).repeat(32)
    a = np.empty((k // 512, 16))
    for p in range(k // 512):
        a[p, :8] = np.random.permutation(np.resize(levels, 8))
        for g in range(8):
            far = levels[np.abs(levels - a[p, g]) >= 10]
            a[p, g + 8] = far[np.random.randint(len(far))]
    return np.exp2(a.ravel()).repeat(32)


def f64(x):
    return np.asarray(x).astype(np.float64)


K, R, M, N = 512, 256, 512, 1024


def setup_inputs():
    n = np.random.standard_normal
    s = mx_kscale(K)[:, None]
    z = mx_kscale(R, 0)
    return {
        "x": (n((K, N)) * s).astype(np.float32),
        "w": (n((K, M)) / np.sqrt(K) / s).astype(np.float32),
        "a": (n((K, R)) / np.sqrt(K) / s * z).astype(np.float32),
        "bb": (n((R, M)) / np.sqrt(R) / z[:, None]).astype(np.float32),
    }


def reference(x, w, a, bb):
    xq = mxq(f64(x), 0, "e4m3")
    z = mxq(f64(a), 0, "e4m3").T @ xq
    y = (mxq(f64(w), 0, "e4m3").T @ xq) + (mxq(f64(bb), 0, "e4m3").T @ mxq(z, 0, "e4m3"))
    y = 1.0 / (1.0 + np.exp(-(y)))
    return y

@@ -1,0 +1,183 @@
+from contextlib import ExitStack
+
+import concourse.mybir as mybir
+
+K, R, M, N = 512, 256, 512, 1024
+FLOPS = 2 * N * (K * M + K * R + R * M)
+
+F32 = mybir.dt.float32
+BF16 = mybir.dt.bfloat16
+I32 = mybir.dt.int32
+U8 = mybir.dt.uint8
+FP8X4 = mybir.dt.float8_e4m3fn_x4
+SIGMOID = mybir.ActivationFunctionType.Sigmoid
+
+P = 128
+H = 64
+W = 256
+REC = W + W // 4
+
+XLOADS = [[0,1],[2],[3]]
+ORDER = """Lw:S La:S Lx01:S LbH:S warm:S Lx2:S cw10:V cw00:S cw11:V cw01:V
+qw1:V ca1:S qw0:V ca0:S sw0:Q LbL:Q sw1:S qa0:V Lx3:S qa1:V
+cx00:S cx01:V cx10:S qx0:V cx11:V mz01:P sx00:Q sx01:Q qx1:V mz00:P
+ez01:S ez00:V mz11:P cb1:S cb0:V mz10:P qz0:V sx10:S ez10:S qb:V
+cx20:V sx11:S my0:P ez11:S cx21:V qx2:V qz1:V sx20:Q mz21:P sg10:S
+sx21:Q cx31:V mz20:P ez21:S st10:Q cx30:V my1:P ez20:S qx3:V sg00:S
+qz2:V mz30:P sx30:Q sx31:Q mz31:P sg01:S st00:Q ez30:V my2:P ez31:S
+st01:Q sg11:S qz3:V sg02:S st11:Q my3:P sg12:S st02:Q st12:Q sg13:S
+sg03:S st13:Q st03:Q """.split()
+
+
+def codes(rec, rows, c0, n):
+    return rec[rows, c0 : c0 + n].bitcast(FP8X4)
+
+
+def scales(rec, rows, c0, n):
+    return rec[rows, W + c0 // 4 : W + (c0 + n) // 4].bitcast(U8)
+
+
+def tile_rows_lora_sigmoid_kernel(tc, x, w, a, bb, out):
+    nc = tc.nc
+    allp = slice(0, P)
+    half = [slice(0, H), slice(H, P)]
+    with ExitStack() as ctx:
+        sb = ctx.enter_context(tc.tile_pool(name="sb", bufs=1))
+        ps = ctx.enter_context(tc.psum_pool(name="ps", bufs=1))
+        ctx.enter_context(tc.manual_schedule())
+
+        a_raw = sb.tile([P, 4, R], F32, name="a_raw", align_bytes=64)
+        w_raw = sb.tile([P, 4, M], F32, name="w_raw", align_bytes=64)
+        b_raw = sb.tile([P, 4, W], F32, name="b_raw", align_bytes=64)
+        x_raw = {}
+        for g in XLOADS:
+            t = sb.tile([P, 4, W * len(g)], F32, name="x_raw%d" % g[0], align_bytes=64)
+            for i, q in enumerate(g):
+                x_raw[q] = (t, i * W, g)
+        a_bf = sb.tile([P, 4, H, 4], BF16, name="a_bf", align_bytes=64)
+        b_bf = sb.tile([P, W, 4], BF16, name="b_bf", align_bytes=64)
+        w_bf = [sb.tile([P, W, 4], BF16, name="w_bf%d" % u, align_bytes=64) for u in range(2)]
+        x_bf = [sb.tile([P, W, 4], BF16, name="x_bf%d" % q, align_bytes=64) for q in range(4)]
+        z_bf = [sb.tile([P, W, 4], BF16, name="z_bf%d" % q, align_bytes=64) for q in range(4)]
+        a_codes = sb.tile([P, 4, 2, H], I32, name="a_codes", align_bytes=64)
+        a_scales = sb.tile([P, 4, 2, H], U8, name="a_scales", align_bytes=64)
+        b_q = sb.tile([P, REC], I32, name="b_q", align_bytes=64)
+        own = sb.tile([P, 6, REC], I32, name="own", align_bytes=64)
+        other = [sb.tile([P, REC], I32, name="other%d" % i, align_bytes=64) for i in range(5)]
+        z_q = [sb.tile([P, REC], I32, name="z_q%d" % q, align_bytes=64) for q in range(4)]
+        res = [[sb.tile([P, 2, W], F32, name="res%d%d" % (u, q), align_bytes=64) for q in range(4)] for u in range(2)]
+        warm = sb.tile([P, 16], F32, name="warm", align_bytes=64)
+        z_ps = [ps.tile([P, 4, P], F32, name="z_ps%d" % i) for i in range(2)]
+        y_ps = [[ps.tile([P, 2, W], F32, name="y_ps%d%d" % (u, i)) for i in range(3)] for u in range(2)]
+        state = {"z": 0, "y": 0}
+        zbank = {}
+        ybank = {}
+
+        nc.vector.memset(warm[:, 0:8], 0.0)
+        nc.vector.memset(own[:, :, W:REC], 0)
+
+        def copy(e, dst, src):
+            if e == "V":
+                nc.vector.tensor_copy(out=dst, in_=src)
+            else:
+                nc.scalar.copy(out=dst, in_=src)
+
+        def cast(e, bf, raw, c0, h):
+            dst = bf[:, h * P : (h + 1) * P, :].rearrange("p (c i) t -> p c t i", i=4)
+            src = raw[:, :, c0 + h * P : c0 + (h + 1) * P].rearrange("p t (c i) -> p c t i", i=4)
+            copy(e, dst, src)
+
+        def quant(rec, bf):
+            nc.vector.quantize_mx(out=codes(rec, allp, 0, W), scales=scales(rec, allp, 0, W), in_=bf[:].rearrange("p n t -> p (n t)"))
+
+        for item in ORDER:
+            name, e = item.split(":")
+            dq = nc.scalar if e == "S" else nc.sync
+            kind = name[:2]
+            d = [int(ch) for ch in name[2:]] if name[0] != "L" and name != "warm" else []
+            if name == "La":
+                dq.dma_start(out=a_raw[:], in_=a.rearrange("(p j) r -> p j r", j=4))
+            elif name == "Lw":
+                dq.dma_start(out=w_raw[:], in_=w.rearrange("(p j) m -> p j m", j=4))
+            elif name == "LbL" or name == "LbH":
+                h = 0 if name == "LbL" else 1
+                dq.dma_start(out=b_raw[half[h]], in_=bb[:, h * W : (h + 1) * W].rearrange("(p j) m -> p j m", j=4))
+            elif kind == "Lx":
+                t, c0, g = x_raw[int(name[2])]
+                dq.dma_start(out=t[:], in_=x[:, g[0] * W : (g[-1] + 1) * W].rearrange("(p j) n -> p j n", j=4))
+            elif name == "warm":
+                nc.scalar.activation(out=warm[:, 8:9], in_=warm[:, 0:1], func=SIGMOID)
+            elif kind == "ca":
+                c0 = 32 * d[0]
+                dst = a_bf[:, :, c0 : c0 + 32, :].rearrange("p i c t -> p c t i")
+                src = a_raw[:, :, 4 * c0 : 4 * c0 + P].rearrange("p t (c i) -> p c t i", i=4)
+                copy(e, dst, src)
+            elif kind == "qa":
+                for j in (2 * d[0], 2 * d[0] + 1):
+                    for h in range(2):
+                        nc.vector.quantize_mx(out=a_codes[:, j, h, :].bitcast(FP8X4), scales=a_scales[:, j, h, :], in_=a_bf[:, j].rearrange("p c t -> p (c t)"))
+            elif kind == "cb":
+                cast(e, b_bf, b_raw, 0, d[0])
+            elif kind == "qb":
+                quant(b_q, b_bf)
+            elif kind == "cw":
+                cast(e, w_bf[d[0]], w_raw, d[0] * W, d[1])
+            elif kind == "qw":
+                quant(own[:, d[0]], w_bf[d[0]])
+            elif kind == "sw":
+                u = d[0]
+                dq.dma_start(out=other[0][half[u]], in_=own[half[1 - u], u])
+            elif kind == "cx":
+                t, c0, g = x_raw[d[0]]
+                cast(e, x_bf[d[0]], t, c0, d[1])
+            elif kind == "qx":
+                quant(own[:, 2 + d[0]], x_bf[d[0]])
+            elif kind == "sx":
+                q, h = d
+                dq.dma_start(out=other[1 + q][half[h]], in_=own[half[1 - h], 2 + q])
+            elif kind == "mz":
+                q, s = d
+                bank = z_ps[state["z"] % 2]
+                state["z"] = state["z"] + 1
+                zbank[(q, s)] = bank
+                for j in range(4):
+                    nc.tensor.matmul_mx(
+                        out=bank[:, j, :],
+                        lhsT=a_codes[:, j].rearrange("p h c -> p (h c)").bitcast(FP8X4),
+                        lhsT_scale=a_scales[:, j].rearrange("p h c -> p (h c)"),
+                        rhs=codes(own[:, 2 + q], allp, s * P, P),
+                        rhs_scale=scales(own[:, 2 + q], allp, s * P, P),
+                        start=True,
+                        stop=True,
+                    )
+            elif kind == "ez":
+                q, s = d
+                copy(e, z_bf[q][:, s * P : (s + 1) * P, :], zbank[(q, s)][:].rearrange("p j n -> p n j"))
+            elif kind == "qz":
+                quant(z_q[d[0]], z_bf[d[0]])
+            elif kind == "my":
+                q = d[0]
+                i = state["y"] % 3
+                state["y"] = state["y"] + 1
+                ybank[q] = i
+                for t in range(2):
+                    for s in range(2):
+                        for k in range(3):
+                            for u in range(2):
+                                lhs = [own[:, u], other[0], b_q][k]
+                                rhs = [own[:, 2 + q], other[1 + q], z_q[q]][k]
+                                nc.tensor.matmul_mx(
+                                    out=y_ps[u][i][:, t, s * P : (s + 1) * P],
+                                    lhsT=codes(lhs, half[u], t * P, P),
+                                    lhsT_scale=scales(lhs, half[u], t * P, P),
+                                    rhs=codes(rhs, half[u], s * P, P),
+                                    rhs_scale=scales(rhs, half[u], s * P, P),
+                                    start=(k == 0),
+                                    stop=(k == 2),
+                                )
+            elif kind == "sg":
+                u, q = d
+                nc.scalar.activation(out=res[u][q][:], in_=y_ps[u][ybank[q]][:], func=SIGMOID)
+            elif kind == "st":
+                u, q = d
+                dq.dma_start(out=out[u * W : (u + 1) * W, q * W : (q + 1) * W].rearrange("(t p) n -> p t n", p=P), in_=res[u][q][:])

@@ -11,6 +11,8 @@ I32 = mybir.dt.int32
 U8 = mybir.dt.uint8
 FP8X4 = mybir.dt.float8_e4m3fn_x4
 SIGMOID = mybir.ActivationFunctionType.Sigmoid
+ADD = mybir.AluOpType.add
+MULT = mybir.AluOpType.mult
 
 P = 128
 H = 64
@@ -18,15 +20,17 @@ W = 256
 REC = W + W // 4
 
 XLOADS = [[0,1],[2],[3]]
-ORDER = """Lw:S La:S Lx01:S LbH:S warm:S Lx2:S cw10:V cw00:S cw11:V cw01:V
-qw1:V ca1:S qw0:V ca0:S sw0:Q LbL:Q sw1:S qa0:V Lx3:S qa1:V
-cx00:S cx01:V cx10:S qx0:V cx11:V mz01:P sx00:Q sx01:Q qx1:V mz00:P
-ez01:S ez00:V mz11:P cb1:S cb0:V mz10:P qz0:V sx10:S ez10:S qb:V
-cx20:V sx11:S my0:P ez11:S cx21:V qx2:V qz1:V sx20:Q mz21:P sg10:S
-sx21:Q cx31:V mz20:P ez21:S st10:Q cx30:V my1:P ez20:S qx3:V sg00:S
-qz2:V mz30:P sx30:Q sx31:Q mz31:P sg01:S st00:Q ez30:V my2:P ez31:S
-st01:Q sg11:S qz3:V sg02:S st11:Q my3:P sg12:S st02:Q st12:Q sg13:S
-sg03:S st13:Q st03:Q """.split()
+WHOLE = True
+ORDER = """warm:S La:Q Lx01:Q Lw:Q LbH:Q LbL:Q Lx2:Q Lx3:Q ca0:S ca1:V
+qa1:V qa0:V cx11:S cx10:V cx01:V cx00:S qx1:V mz1:P qx0:V mz0:P
+cw00:S cw11:V cw10:V cw01:V ez1:S qw1:V ez0:S qw0:V m110:P qz1:V
+cb1:S cb0:V m100:P cp10:V cp00:S qb:V m101:P m111:P wz008:P cx21:V sb1:S
+cp01:S cx20:V qz0:V sb0:S qx2:V cp11:S cx30:V mz2:P cx31:S m211:P
+ez2:S qx3:V m112:P ad11:V m201:P cp12:S m102:P qz2:V ad01:V m210:P
+cp02:S m200:P ad10:V m202:P sg11:S m103:P ad00:V mz3:P sg01:S st11:Q
+ad02:V sg10:S m113:P st01:Q ez3:V m212:P sg00:S st10:Q ad12:V cp03:S
+st00:Q qz3:V cp13:V sg12:S n2013:P n2003:P n2113:P sg02:S bd013:V st12:Q
+n2103:P bd003:V bd113:V st02:Q sg03:S bd103:V sg13:S st03:Q st13:Q """.split()
 
 
 def codes(rec, rows, c0, n):
@@ -47,7 +51,11 @@ def tile_rows_lora_sigmoid_kernel(tc, x, w, a, bb, out):
         ctx.enter_context(tc.manual_schedule())
 
         a_raw = sb.tile([P, 4, R], F32, name="a_raw", align_bytes=64)
-        w_raw = sb.tile([P, 4, M], F32, name="w_raw", align_bytes=64)
+        if WHOLE:
+            w_all = sb.tile([P, 4, M], F32, name="w_all", align_bytes=64)
+            w_raw = [(w_all, 0), (w_all, W)]
+        else:
+            w_raw = [(sb.tile([P, 4, W], F32, name="w_raw%d" % u, align_bytes=64), 0) for u in range(2)]
         b_raw = sb.tile([P, 4, W], F32, name="b_raw", align_bytes=64)
         x_raw = {}
         for g in XLOADS:
@@ -58,37 +66,60 @@ def tile_rows_lora_sigmoid_kernel(tc, x, w, a, bb, out):
         b_bf = sb.tile([P, W, 4], BF16, name="b_bf", align_bytes=64)
         w_bf = [sb.tile([P, W, 4], BF16, name="w_bf%d" % u, align_bytes=64) for u in range(2)]
         x_bf = [sb.tile([P, W, 4], BF16, name="x_bf%d" % q, align_bytes=64) for q in range(4)]
-        z_bf = [sb.tile([P, W, 4], BF16, name="z_bf%d" % q, align_bytes=64) for q in range(4)]
-        a_codes = sb.tile([P, 4, 2, H], I32, name="a_codes", align_bytes=64)
-        a_scales = sb.tile([P, 4, 2, H], U8, name="a_scales", align_bytes=64)
-        b_q = sb.tile([P, REC], I32, name="b_q", align_bytes=64)
-        own = sb.tile([P, 6, REC], I32, name="own", align_bytes=64)
-        other = [sb.tile([P, REC], I32, name="other%d" % i, align_bytes=64) for i in range(5)]
+        z_bf = [sb.tile([P, P, 4], BF16, name="z_bf%d" % q, align_bytes=64) for q in range(4)]
+        a_codes = sb.tile([P, 9 * H], I32, name="a_codes", align_bytes=64)
+        a_scales = sb.tile([P, 9 * H], U8, name="a_scales", align_bytes=64)
+        b_own = sb.tile([P, REC], I32, name="b_own", align_bytes=64)
+        b_other = sb.tile([P, REC], I32, name="b_other", align_bytes=64)
+        w_q = [sb.tile([P, REC], I32, name="w_q%d" % u, align_bytes=64) for u in range(2)]
+        x_q = [sb.tile([P, REC], I32, name="x_q%d" % q, align_bytes=64) for q in range(4)]
         z_q = [sb.tile([P, REC], I32, name="z_q%d" % q, align_bytes=64) for q in range(4)]
+        part = [sb.tile([P, 4, W], F32, name="part%d" % q, align_bytes=64) for q in range(4)]
+        total = [sb.tile([P, 4, W], F32, name="total%d" % q, align_bytes=64) for q in range(4)]
         res = [[sb.tile([P, 2, W], F32, name="res%d%d" % (u, q), align_bytes=64) for q in range(4)] for u in range(2)]
         warm = sb.tile([P, 16], F32, name="warm", align_bytes=64)
         z_ps = [ps.tile([P, 4, P], F32, name="z_ps%d" % i) for i in range(2)]
-        y_ps = [[ps.tile([P, 2, W], F32, name="y_ps%d%d" % (u, i)) for i in range(3)] for u in range(2)]
-        state = {"z": 0, "y": 0}
-        zbank = {}
-        ybank = {}
+        y1_ps = [ps.tile([P, 2, W], F32, name="y1_ps%d" % i) for i in range(2)]
+        y2_ps = [[ps.tile([P, 4, P], F32, name="y2_ps%d%d" % (h, i)) for i in range(2)] for h in range(2)]
+        count = {"z": 0, "y1": 0, 0: 0, 1: 0}
+        bank_of = {}
 
         nc.vector.memset(warm[:, 0:8], 0.0)
-        nc.vector.memset(own[:, :, W:REC], 0)
+        nc.vector.memset(b_own[:, W:REC], 0)
+        nc.vector.memset(a_codes[:], 0)
+        nc.vector.memset(a_scales[:].bitcast(I32), 0)
+
+        def take(pool, key):
+            bank = pool[count[key] % 2]
+            count[key] = count[key] + 1
+            return bank
 
         def copy(e, dst, src):
             if e == "V":
                 nc.vector.tensor_copy(out=dst, in_=src)
-            else:
+            elif e == "S":
                 nc.scalar.copy(out=dst, in_=src)
+            else:
+                nc.gpsimd.tensor_scalar(out=dst, in0=src, scalar1=1.0, scalar2=0.0, op0=MULT, op1=ADD)
 
         def cast(e, bf, raw, c0, h):
             dst = bf[:, h * P : (h + 1) * P, :].rearrange("p (c i) t -> p c t i", i=4)
             src = raw[:, :, c0 + h * P : c0 + (h + 1) * P].rearrange("p t (c i) -> p c t i", i=4)
             copy(e, dst, src)
 
-        def quant(rec, bf):
-            nc.vector.quantize_mx(out=codes(rec, allp, 0, W), scales=scales(rec, allp, 0, W), in_=bf[:].rearrange("p n t -> p (n t)"))
+        def quant(rec, bf, n):
+            nc.vector.quantize_mx(out=codes(rec, allp, 0, n), scales=scales(rec, allp, 0, n), in_=bf[:].rearrange("p n t -> p (n t)"))
+
+        def mm(dst, lhs, lc, rhs, rc, rows):
+            nc.tensor.matmul_mx(
+                out=dst,
+                lhsT=codes(lhs, rows, lc, P),
+                lhsT_scale=scales(lhs, rows, lc, P),
+                rhs=codes(rhs, rows, rc, P),
+                rhs_scale=scales(rhs, rows, rc, P),
+                start=True,
+                stop=True,
+            )
 
         for item in ORDER:
             name, e = item.split(":")
@@ -98,7 +129,10 @@ def tile_rows_lora_sigmoid_kernel(tc, x, w, a, bb, out):
             if name == "La":
                 dq.dma_start(out=a_raw[:], in_=a.rearrange("(p j) r -> p j r", j=4))
             elif name == "Lw":
-                dq.dma_start(out=w_raw[:], in_=w.rearrange("(p j) m -> p j m", j=4))
+                dq.dma_start(out=w_raw[0][0][:], in_=w.rearrange("(p j) m -> p j m", j=4))
+            elif kind == "Lw":
+                u = int(name[2])
+                dq.dma_start(out=w_raw[u][0][:], in_=w[:, u * W : (u + 1) * W].rearrange("(p j) m -> p j m", j=4))
             elif name == "LbL" or name == "LbH":
                 h = 0 if name == "LbL" else 1
                 dq.dma_start(out=b_raw[half[h]], in_=bb[:, h * W : (h + 1) * W].rearrange("(p j) m -> p j m", j=4))
@@ -114,70 +148,92 @@ def tile_rows_lora_sigmoid_kernel(tc, x, w, a, bb, out):
                 copy(e, dst, src)
             elif kind == "qa":
                 for j in (2 * d[0], 2 * d[0] + 1):
-                    for h in range(2):
-                        nc.vector.quantize_mx(out=a_codes[:, j, h, :].bitcast(FP8X4), scales=a_scales[:, j, h, :], in_=a_bf[:, j].rearrange("p c t -> p (c t)"))
+                    c0 = H + P * j
+                    nc.vector.quantize_mx(out=a_codes[:, c0 : c0 + H].bitcast(FP8X4), scales=a_scales[:, c0 : c0 + H], in_=a_bf[:, j].rearrange("p c t -> p (c t)"))
             elif kind == "cb":
                 cast(e, b_bf, b_raw, 0, d[0])
             elif kind == "qb":
-                quant(b_q, b_bf)
+                quant(b_own, b_bf, W)
+            elif kind == "sb":
+                h = d[0]
+                dq.dma_start(out=b_other[half[h]], in_=b_own[half[1 - h]])
             elif kind == "cw":
-                cast(e, w_bf[d[0]], w_raw, d[0] * W, d[1])
+                cast(e, w_bf[d[0]], w_raw[d[0]][0], w_raw[d[0]][1], d[1])
             elif kind == "qw":
-                quant(own[:, d[0]], w_bf[d[0]])
-            elif kind == "sw":
-                u = d[0]
-                dq.dma_start(out=other[0][half[u]], in_=own[half[1 - u], u])
+                quant(w_q[d[0]], w_bf[d[0]], W)
             elif kind == "cx":
                 t, c0, g = x_raw[d[0]]
                 cast(e, x_bf[d[0]], t, c0, d[1])
             elif kind == "qx":
-                quant(own[:, 2 + d[0]], x_bf[d[0]])
-            elif kind == "sx":
-                q, h = d
-                dq.dma_start(out=other[1 + q][half[h]], in_=own[half[1 - h], 2 + q])
+                quant(x_q[d[0]], x_bf[d[0]], W)
+            elif kind == "wz" or kind == "wy":
+                src = [w_q[0], w_q[1], b_own, x_q[0]][d[0]]
+                bank = z_ps[count["z"] % 2][:, 0, :] if kind == "wz" else y1_ps[count["y1"] % 2][:, 0, 0:P]
+                for i in range(10 * d[1] + d[2]):
+                    mm(bank, src, 0, src, P, allp)
             elif kind == "mz":
-                q, s = d
-                bank = z_ps[state["z"] % 2]
-                state["z"] = state["z"] + 1
-                zbank[(q, s)] = bank
-                for j in range(4):
-                    nc.tensor.matmul_mx(
-                        out=bank[:, j, :],
-                        lhsT=a_codes[:, j].rearrange("p h c -> p (h c)").bitcast(FP8X4),
-                        lhsT_scale=a_scales[:, j].rearrange("p h c -> p (h c)"),
-                        rhs=codes(own[:, 2 + q], allp, s * P, P),
-                        rhs_scale=scales(own[:, 2 + q], allp, s * P, P),
-                        start=True,
-                        stop=True,
-                    )
-            elif kind == "ez":
-                q, s = d
-                copy(e, z_bf[q][:, s * P : (s + 1) * P, :], zbank[(q, s)][:].rearrange("p j n -> p n j"))
-            elif kind == "qz":
-                quant(z_q[d[0]], z_bf[d[0]])
-            elif kind == "my":
                 q = d[0]
-                i = state["y"] % 3
-                state["y"] = state["y"] + 1
-                ybank[q] = i
+                bank = take(z_ps, "z")
+                bank_of[name] = bank
+                for j in range(4):
+                    for h in range(2):
+                        c0 = P * j + H * (1 - h)
+                        nc.tensor.matmul_mx(
+                            out=bank[:, j, :],
+                            lhsT=a_codes[:, c0 : c0 + P].bitcast(FP8X4),
+                            lhsT_scale=a_scales[:, c0 : c0 + P],
+                            rhs=codes(x_q[q], allp, h * P, P),
+                            rhs_scale=scales(x_q[q], allp, h * P, P),
+                            start=(h == 0),
+                            stop=(h == 1),
+                        )
+            elif kind == "ez":
+                q = d[0]
+                copy(e, z_bf[q][:], bank_of["mz%d" % q][:].rearrange("p j n -> p n j"))
+            elif kind == "qz":
+                quant(z_q[d[0]], z_bf[d[0]], P)
+            elif kind == "m1":
+                u, q = d
+                bank = take(y1_ps, "y1")
+                bank_of[name] = bank
                 for t in range(2):
                     for s in range(2):
-                        for k in range(3):
-                            for u in range(2):
-                                lhs = [own[:, u], other[0], b_q][k]
-                                rhs = [own[:, 2 + q], other[1 + q], z_q[q]][k]
-                                nc.tensor.matmul_mx(
-                                    out=y_ps[u][i][:, t, s * P : (s + 1) * P],
-                                    lhsT=codes(lhs, half[u], t * P, P),
-                                    lhsT_scale=scales(lhs, half[u], t * P, P),
-                                    rhs=codes(rhs, half[u], s * P, P),
-                                    rhs_scale=scales(rhs, half[u], s * P, P),
-                                    start=(k == 0),
-                                    stop=(k == 2),
-                                )
+                        mm(bank[:, t, s * P : (s + 1) * P], w_q[u], t * P, x_q[q], s * P, allp)
+            elif kind == "cp":
+                u, q = d
+                copy(e, part[q][:, 2 * u : 2 * u + 2, :], bank_of["m1%d%d" % (u, q)][:])
+            elif kind == "m2":
+                h, q = d
+                bank = take(y2_ps[h], h)
+                bank_of[name] = bank
+                for u in range(2):
+                    for t in range(2):
+                        mm(bank[:, 2 * u + t, :], b_own if u == h else b_other, t * P, z_q[q], 0, half[h])
+            elif kind == "n2":
+                u, h, q = d
+                bank = take(y2_ps[h], h)
+                bank_of[name] = bank
+                for t in range(2):
+                    mm(bank[:, t, :], b_own if u == h else b_other, t * P, z_q[q], 0, half[h])
+            elif kind == "ad":
+                h, q = d
+                cols = slice(h * P, (h + 1) * P)
+                nc.vector.tensor_tensor(out=total[q][:, :, cols], in0=bank_of["m2%d%d" % (h, q)][:], in1=part[q][:, :, cols], op=ADD)
+            elif kind == "bd":
+                u, h, q = d
+                cols = slice(h * P, (h + 1) * P)
+                rows = slice(2 * u, 2 * u + 2)
+                nc.vector.tensor_tensor(out=total[q][:, rows, cols], in0=bank_of["n2%d%d%d" % (u, h, q)][:, 0:2, :], in1=part[q][:, rows, cols], op=ADD)
+            elif kind == "dp":
+                h, q = d
+                copy(e, part[q][:, :, h * P : (h + 1) * P], bank_of["m2%d%d" % (h, q)][:])
+            elif kind == "ae":
+                u, q = d
+                rows = slice(2 * u, 2 * u + 2)
+                nc.vector.tensor_tensor(out=total[q][:, rows, :], in0=bank_of["m1%d%d" % (u, q)][:], in1=part[q][:, rows, :], op=ADD)
             elif kind == "sg":
                 u, q = d
-                nc.scalar.activation(out=res[u][q][:], in_=y_ps[u][ybank[q]][:], func=SIGMOID)
+                nc.scalar.activation(out=res[u][q][:], in_=total[q][:, 2 * u : 2 * u + 2, :], func=SIGMOID)
             elif kind == "st":
                 u, q = d
                 dq.dma_start(out=out[u * W : (u + 1) * W, q * W : (q + 1) * W].rearrange("(t p) n -> p t n", p=P), in_=res[u][q][:])

@@ -3,7 +3,7 @@ from contextlib import ExitStack
 import concourse.mybir as mybir
 
 K, R, M, N = 512, 256, 512, 1024
-FLOPS = 2 * N * (K * M + K * R + R * M)
+FLOPS = 2 * N * (K * R + K * M + R * M)
 
 F32 = mybir.dt.float32
 BF16 = mybir.dt.bfloat16
@@ -12,228 +12,324 @@ U8 = mybir.dt.uint8
 FP8X4 = mybir.dt.float8_e4m3fn_x4
 SIGMOID = mybir.ActivationFunctionType.Sigmoid
 ADD = mybir.AluOpType.add
-MULT = mybir.AluOpType.mult
 
 P = 128
-H = 64
-W = 256
-REC = W + W // 4
-
-XLOADS = [[0,1],[2],[3]]
-WHOLE = True
-ORDER = """warm:S La:Q Lx01:Q Lw:Q LbH:Q LbL:Q Lx2:Q Lx3:Q ca0:S ca1:V
-qa1:V qa0:V cx11:S cx10:V cx01:V cx00:S qx1:V mz1:P qx0:V mz0:P
-cw00:S cw11:V cw10:V cw01:V ez1:S qw1:V ez0:S qw0:V m110:P qz1:V
-cb1:S cb0:V m100:P cp10:V cp00:S qb:V m101:P m111:P wz008:P cx21:V sb1:S
-cp01:S cx20:V qz0:V sb0:S qx2:V cp11:S cx30:V mz2:P cx31:S m211:P
-ez2:S qx3:V m112:P ad11:V m201:P cp12:S m102:P qz2:V ad01:V m210:P
-cp02:S m200:P ad10:V m202:P sg11:S m103:P ad00:V mz3:P sg01:S st11:Q
-ad02:V sg10:S m113:P st01:Q ez3:V m212:P sg00:S st10:Q ad12:V cp03:S
-st00:Q qz3:V cp13:V sg12:S n2013:P n2003:P n2113:P sg02:S bd013:V st12:Q
-n2103:P bd003:V bd113:V st02:Q sg03:S bd103:V sg13:S st03:Q st13:Q """.split()
+HALF = 64
+PACK = 4
+WIDE = 256
+ALIGN = 64
+ALL_ROWS = slice(0, P)
+ROW_TILE = (slice(0, HALF), slice(HALF, P))
 
 
-def codes(rec, rows, c0, n):
-    return rec[rows, c0 : c0 + n].bitcast(FP8X4)
+def record_words(columns):
+    return columns + columns // PACK
 
 
-def scales(rec, rows, c0, n):
-    return rec[rows, W + c0 // 4 : W + (c0 + n) // 4].bitcast(U8)
+def codes(record, rows, first, count):
+    return record[rows, first : first + count].bitcast(FP8X4)
+
+
+def scales(record, rows, first, count):
+    columns = record.shape[-1] * PACK // (PACK + 1)
+    return record[rows, columns + first // PACK : columns + (first + count) // PACK].bitcast(U8)
+
+
+def block(i):
+    return slice(i * P, (i + 1) * P)
 
 
 def tile_rows_lora_sigmoid_kernel(tc, x, w, a, bb, out):
     nc = tc.nc
-    allp = slice(0, P)
-    half = [slice(0, H), slice(H, P)]
     with ExitStack() as ctx:
         sb = ctx.enter_context(tc.tile_pool(name="sb", bufs=1))
         ps = ctx.enter_context(tc.psum_pool(name="ps", bufs=1))
         ctx.enter_context(tc.manual_schedule())
 
-        a_raw = sb.tile([P, 4, R], F32, name="a_raw", align_bytes=64)
-        if WHOLE:
-            w_all = sb.tile([P, 4, M], F32, name="w_all", align_bytes=64)
-            w_raw = [(w_all, 0), (w_all, W)]
-        else:
-            w_raw = [(sb.tile([P, 4, W], F32, name="w_raw%d" % u, align_bytes=64), 0) for u in range(2)]
-        b_raw = sb.tile([P, 4, W], F32, name="b_raw", align_bytes=64)
-        x_raw = {}
-        for g in XLOADS:
-            t = sb.tile([P, 4, W * len(g)], F32, name="x_raw%d" % g[0], align_bytes=64)
-            for i, q in enumerate(g):
-                x_raw[q] = (t, i * W, g)
-        a_bf = sb.tile([P, 4, H, 4], BF16, name="a_bf", align_bytes=64)
-        b_bf = sb.tile([P, W, 4], BF16, name="b_bf", align_bytes=64)
-        w_bf = [sb.tile([P, W, 4], BF16, name="w_bf%d" % u, align_bytes=64) for u in range(2)]
-        x_bf = [sb.tile([P, W, 4], BF16, name="x_bf%d" % q, align_bytes=64) for q in range(4)]
-        z_bf = [sb.tile([P, P, 4], BF16, name="z_bf%d" % q, align_bytes=64) for q in range(4)]
-        a_codes = sb.tile([P, 9 * H], I32, name="a_codes", align_bytes=64)
-        a_scales = sb.tile([P, 9 * H], U8, name="a_scales", align_bytes=64)
-        b_own = sb.tile([P, REC], I32, name="b_own", align_bytes=64)
-        b_other = sb.tile([P, REC], I32, name="b_other", align_bytes=64)
-        w_q = [sb.tile([P, REC], I32, name="w_q%d" % u, align_bytes=64) for u in range(2)]
-        x_q = [sb.tile([P, REC], I32, name="x_q%d" % q, align_bytes=64) for q in range(4)]
-        z_q = [sb.tile([P, REC], I32, name="z_q%d" % q, align_bytes=64) for q in range(4)]
-        part = [sb.tile([P, 4, W], F32, name="part%d" % q, align_bytes=64) for q in range(4)]
-        total = [sb.tile([P, 4, W], F32, name="total%d" % q, align_bytes=64) for q in range(4)]
-        res = [[sb.tile([P, 2, W], F32, name="res%d%d" % (u, q), align_bytes=64) for q in range(4)] for u in range(2)]
-        warm = sb.tile([P, 16], F32, name="warm", align_bytes=64)
-        z_ps = [ps.tile([P, 4, P], F32, name="z_ps%d" % i) for i in range(2)]
-        y1_ps = [ps.tile([P, 2, W], F32, name="y1_ps%d" % i) for i in range(2)]
-        y2_ps = [[ps.tile([P, 4, P], F32, name="y2_ps%d%d" % (h, i)) for i in range(2)] for h in range(2)]
-        count = {"z": 0, "y1": 0, 0: 0, 1: 0}
-        bank_of = {}
+        def tiles(name, count, shape, dtype):
+            return [sb.tile(shape, dtype, name="%s%d" % (name, i), align_bytes=ALIGN) for i in range(count)]
 
-        nc.vector.memset(warm[:, 0:8], 0.0)
-        nc.vector.memset(b_own[:, W:REC], 0)
-        nc.vector.memset(a_codes[:], 0)
-        nc.vector.memset(a_scales[:].bitcast(I32), 0)
+        a_raw = sb.tile([P, PACK, R], F32, name="a_raw", align_bytes=ALIGN)
+        bb_raw = sb.tile([P, PACK, WIDE], F32, name="bb_raw", align_bytes=ALIGN)
+        w_raw = tiles("w_raw", 2, [P, PACK, WIDE], F32)
+        x_early = sb.tile([P, PACK, 2 * WIDE], F32, name="x_early", align_bytes=ALIGN)
+        x_late = tiles("x_late", 2, [P, PACK, WIDE], F32)
+        x_raw = [x_early[:, :, 0:WIDE], x_early[:, :, WIDE : 2 * WIDE], x_late[0][:], x_late[1][:]]
 
-        def take(pool, key):
-            bank = pool[count[key] % 2]
-            count[key] = count[key] + 1
-            return bank
+        a_bf = sb.tile([P, PACK, HALF, PACK], BF16, name="a_bf", align_bytes=ALIGN)
+        bb_bf = sb.tile([P, WIDE, PACK], BF16, name="bb_bf", align_bytes=ALIGN)
+        w_bf = tiles("w_bf", 2, [P, WIDE, PACK], BF16)
+        x_bf = tiles("x_bf", 4, [P, WIDE, PACK], BF16)
+        z_bf = tiles("z_bf", 4, [P, P, PACK], BF16)
 
-        def copy(e, dst, src):
-            if e == "V":
+        a_codes = sb.tile([P, (2 * PACK + 1) * HALF], I32, name="a_codes", align_bytes=ALIGN)
+        a_scales = sb.tile([P, (2 * PACK + 1) * HALF], U8, name="a_scales", align_bytes=ALIGN)
+        bb_own = sb.tile([P, record_words(WIDE)], I32, name="bb_own", align_bytes=ALIGN)
+        bb_far = sb.tile([P, record_words(WIDE)], I32, name="bb_far", align_bytes=ALIGN)
+        w_own = tiles("w_own", 2, [P, record_words(WIDE)], I32)
+        w_far = tiles("w_far", 2, [P, record_words(WIDE)], I32)
+        x_own = tiles("x_own", 4, [P, 2, record_words(P)], I32)
+        x_far = dict(zip((2, 3), tiles("x_far", 2, [P, record_words(P)], I32)))
+        z_rec = tiles("z_rec", 4, [P, record_words(P)], I32)
+
+        wx = [tiles("wx%d_" % q, 2, [P, 2, WIDE], F32) for q in range(2)]
+        y_sum = [tiles("y_sum%d_" % q, 2, [P, 2, WIDE], F32) for q in range(2)]
+        result = [tiles("result%d_" % q, 2, [P, 2, WIDE], F32) for q in range(4)]
+        warm_up = sb.tile([P, 16], F32, name="warm_up", align_bytes=ALIGN)
+
+        z_bank = [ps.tile([P, PACK, P], F32, name="z_bank%d" % i) for i in range(2)]
+        wx_bank = [ps.tile([P, 2, WIDE], F32, name="wx_bank%d" % q) for q in range(2)]
+        y_bank = [[ps.tile([P, 2, P], F32, name="y_bank%d%d" % (h, u)) for u in range(2)] for h in range(2)]
+
+        def copy(engine, dst, src):
+            if engine is nc.vector:
                 nc.vector.tensor_copy(out=dst, in_=src)
-            elif e == "S":
-                nc.scalar.copy(out=dst, in_=src)
             else:
-                nc.gpsimd.tensor_scalar(out=dst, in0=src, scalar1=1.0, scalar2=0.0, op0=MULT, op1=ADD)
+                nc.scalar.copy(out=dst, in_=src)
 
-        def cast(e, bf, raw, c0, h):
-            dst = bf[:, h * P : (h + 1) * P, :].rearrange("p (c i) t -> p c t i", i=4)
-            src = raw[:, :, c0 + h * P : c0 + (h + 1) * P].rearrange("p t (c i) -> p c t i", i=4)
-            copy(e, dst, src)
-
-        def quant(rec, bf, n):
-            nc.vector.quantize_mx(out=codes(rec, allp, 0, n), scales=scales(rec, allp, 0, n), in_=bf[:].rearrange("p n t -> p (n t)"))
-
-        def mm(dst, lhs, lc, rhs, rc, rows):
-            nc.tensor.matmul_mx(
-                out=dst,
-                lhsT=codes(lhs, rows, lc, P),
-                lhsT_scale=scales(lhs, rows, lc, P),
-                rhs=codes(rhs, rows, rc, P),
-                rhs_scale=scales(rhs, rows, rc, P),
-                start=True,
-                stop=True,
+        def interleave(engine, dst, src):
+            copy(
+                engine,
+                dst.rearrange("p (c i) j -> p c j i", i=PACK),
+                src.rearrange("p j (c i) -> p c j i", i=PACK),
             )
 
-        for item in ORDER:
-            name, e = item.split(":")
-            dq = nc.scalar if e == "S" else nc.sync
-            kind = name[:2]
-            d = [int(ch) for ch in name[2:]] if name[0] != "L" and name != "warm" else []
-            if name == "La":
-                dq.dma_start(out=a_raw[:], in_=a.rearrange("(p j) r -> p j r", j=4))
-            elif name == "Lw":
-                dq.dma_start(out=w_raw[0][0][:], in_=w.rearrange("(p j) m -> p j m", j=4))
-            elif kind == "Lw":
-                u = int(name[2])
-                dq.dma_start(out=w_raw[u][0][:], in_=w[:, u * W : (u + 1) * W].rearrange("(p j) m -> p j m", j=4))
-            elif name == "LbL" or name == "LbH":
-                h = 0 if name == "LbL" else 1
-                dq.dma_start(out=b_raw[half[h]], in_=bb[:, h * W : (h + 1) * W].rearrange("(p j) m -> p j m", j=4))
-            elif kind == "Lx":
-                t, c0, g = x_raw[int(name[2])]
-                dq.dma_start(out=t[:], in_=x[:, g[0] * W : (g[-1] + 1) * W].rearrange("(p j) n -> p j n", j=4))
-            elif name == "warm":
-                nc.scalar.activation(out=warm[:, 8:9], in_=warm[:, 0:1], func=SIGMOID)
-            elif kind == "ca":
-                c0 = 32 * d[0]
-                dst = a_bf[:, :, c0 : c0 + 32, :].rearrange("p i c t -> p c t i")
-                src = a_raw[:, :, 4 * c0 : 4 * c0 + P].rearrange("p t (c i) -> p c t i", i=4)
-                copy(e, dst, src)
-            elif kind == "qa":
-                for j in (2 * d[0], 2 * d[0] + 1):
-                    c0 = H + P * j
-                    nc.vector.quantize_mx(out=a_codes[:, c0 : c0 + H].bitcast(FP8X4), scales=a_scales[:, c0 : c0 + H], in_=a_bf[:, j].rearrange("p c t -> p (c t)"))
-            elif kind == "cb":
-                cast(e, b_bf, b_raw, 0, d[0])
-            elif kind == "qb":
-                quant(b_own, b_bf, W)
-            elif kind == "sb":
-                h = d[0]
-                dq.dma_start(out=b_other[half[h]], in_=b_own[half[1 - h]])
-            elif kind == "cw":
-                cast(e, w_bf[d[0]], w_raw[d[0]][0], w_raw[d[0]][1], d[1])
-            elif kind == "qw":
-                quant(w_q[d[0]], w_bf[d[0]], W)
-            elif kind == "cx":
-                t, c0, g = x_raw[d[0]]
-                cast(e, x_bf[d[0]], t, c0, d[1])
-            elif kind == "qx":
-                quant(x_q[d[0]], x_bf[d[0]], W)
-            elif kind == "wz" or kind == "wy":
-                src = [w_q[0], w_q[1], b_own, x_q[0]][d[0]]
-                bank = z_ps[count["z"] % 2][:, 0, :] if kind == "wz" else y1_ps[count["y1"] % 2][:, 0, 0:P]
-                for i in range(10 * d[1] + d[2]):
-                    mm(bank, src, 0, src, P, allp)
-            elif kind == "mz":
-                q = d[0]
-                bank = take(z_ps, "z")
-                bank_of[name] = bank
-                for j in range(4):
-                    for h in range(2):
-                        c0 = P * j + H * (1 - h)
-                        nc.tensor.matmul_mx(
-                            out=bank[:, j, :],
-                            lhsT=a_codes[:, c0 : c0 + P].bitcast(FP8X4),
-                            lhsT_scale=a_scales[:, c0 : c0 + P],
-                            rhs=codes(x_q[q], allp, h * P, P),
-                            rhs_scale=scales(x_q[q], allp, h * P, P),
-                            start=(h == 0),
-                            stop=(h == 1),
-                        )
-            elif kind == "ez":
-                q = d[0]
-                copy(e, z_bf[q][:], bank_of["mz%d" % q][:].rearrange("p j n -> p n j"))
-            elif kind == "qz":
-                quant(z_q[d[0]], z_bf[d[0]], P)
-            elif kind == "m1":
-                u, q = d
-                bank = take(y1_ps, "y1")
-                bank_of[name] = bank
-                for t in range(2):
-                    for s in range(2):
-                        mm(bank[:, t, s * P : (s + 1) * P], w_q[u], t * P, x_q[q], s * P, allp)
-            elif kind == "cp":
-                u, q = d
-                copy(e, part[q][:, 2 * u : 2 * u + 2, :], bank_of["m1%d%d" % (u, q)][:])
-            elif kind == "m2":
-                h, q = d
-                bank = take(y2_ps[h], h)
-                bank_of[name] = bank
-                for u in range(2):
-                    for t in range(2):
-                        mm(bank[:, 2 * u + t, :], b_own if u == h else b_other, t * P, z_q[q], 0, half[h])
-            elif kind == "n2":
-                u, h, q = d
-                bank = take(y2_ps[h], h)
-                bank_of[name] = bank
-                for t in range(2):
-                    mm(bank[:, t, :], b_own if u == h else b_other, t * P, z_q[q], 0, half[h])
-            elif kind == "ad":
-                h, q = d
-                cols = slice(h * P, (h + 1) * P)
-                nc.vector.tensor_tensor(out=total[q][:, :, cols], in0=bank_of["m2%d%d" % (h, q)][:], in1=part[q][:, :, cols], op=ADD)
-            elif kind == "bd":
-                u, h, q = d
-                cols = slice(h * P, (h + 1) * P)
-                rows = slice(2 * u, 2 * u + 2)
-                nc.vector.tensor_tensor(out=total[q][:, rows, cols], in0=bank_of["n2%d%d%d" % (u, h, q)][:, 0:2, :], in1=part[q][:, rows, cols], op=ADD)
-            elif kind == "dp":
-                h, q = d
-                copy(e, part[q][:, :, h * P : (h + 1) * P], bank_of["m2%d%d" % (h, q)][:])
-            elif kind == "ae":
-                u, q = d
-                rows = slice(2 * u, 2 * u + 2)
-                nc.vector.tensor_tensor(out=total[q][:, rows, :], in0=bank_of["m1%d%d" % (u, q)][:], in1=part[q][:, rows, :], op=ADD)
-            elif kind == "sg":
-                u, q = d
-                nc.scalar.activation(out=res[u][q][:], in_=total[q][:, 2 * u : 2 * u + 2, :], func=SIGMOID)
-            elif kind == "st":
-                u, q = d
-                dq.dma_start(out=out[u * W : (u + 1) * W, q * W : (q + 1) * W].rearrange("(t p) n -> p t n", p=P), in_=res[u][q][:])
+        def quantize(record, count, values):
+            nc.vector.quantize_mx(
+                out=codes(record, ALL_ROWS, 0, count),
+                scales=scales(record, ALL_ROWS, 0, count),
+                in_=values.rearrange("p c j -> p (c j)"),
+            )
+
+        def multiply(dst, rows, lhs, lhs_first, rhs, start=True, stop=True):
+            nc.tensor.matmul_mx(
+                out=dst,
+                lhsT=codes(lhs, rows, lhs_first, P),
+                lhsT_scale=scales(lhs, rows, lhs_first, P),
+                rhs=codes(rhs, rows, 0, P),
+                rhs_scale=scales(rhs, rows, 0, P),
+                start=start,
+                stop=stop,
+            )
+
+        def load(queue, dst, src):
+            queue.dma_start(out=dst, in_=src.rearrange("(p j) c -> p j c", j=PACK))
+
+        def bring_over(queue, far, own, h):
+            queue.dma_start(out=far[ROW_TILE[h]], in_=own[ROW_TILE[1 - h]])
+
+        def round_a(h):
+            nc.vector.tensor_copy(
+                out=a_bf[:, :, 32 * h : 32 * (h + 1), :].rearrange("p i c j -> p c j i"),
+                in_=a_raw[:, :, block(h)].rearrange("p j (c i) -> p c j i", i=PACK),
+            )
+
+        def quantize_a(j):
+            columns = slice(HALF + P * j, P + P * j)
+            nc.vector.quantize_mx(
+                out=a_codes[:, columns].bitcast(FP8X4),
+                scales=a_scales[:, columns],
+                in_=a_bf[:, j].rearrange("p c i -> p (c i)"),
+            )
+
+        def round_w(engine, u, t):
+            interleave(engine, w_bf[u][:, block(t), :], w_raw[u][:, :, block(t)])
+
+        def round_x(engine, q, h):
+            interleave(engine, x_bf[q][:, block(h), :], x_raw[q][:, :, block(h)])
+
+        def quantize_x(q, h):
+            quantize(x_own[q][:, h], P, x_bf[q][:, block(h), :])
+
+        def z_product(q):
+            for j in range(PACK):
+                for h in range(2):
+                    columns = slice(P * j + HALF * (1 - h), P * (j + 1) + HALF * (1 - h))
+                    nc.tensor.matmul_mx(
+                        out=z_bank[q % 2][:, j, :],
+                        lhsT=a_codes[:, columns].bitcast(FP8X4),
+                        lhsT_scale=a_scales[:, columns],
+                        rhs=codes(x_own[q][:, h], ALL_ROWS, 0, P),
+                        rhs_scale=scales(x_own[q][:, h], ALL_ROWS, 0, P),
+                        start=(h == 0),
+                        stop=(h == 1),
+                    )
+
+        def round_z(engine, q):
+            interleave(engine, z_bf[q][:], z_bank[q % 2][:])
+
+        def quantize_z(q):
+            quantize(z_rec[q], P, z_bf[q][:])
+
+        def bb_record(u, h):
+            return bb_own if u == h else bb_far
+
+        def wx_product(q, u):
+            for t in range(2):
+                for h in range(2):
+                    multiply(wx_bank[q][:, t, block(h)], ALL_ROWS, w_own[u], t * P, x_own[q][:, h])
+
+        def wx_copy(q, u):
+            nc.scalar.copy(out=wx[q][u][:], in_=wx_bank[q][:])
+
+        def lora_product(q, u, h):
+            for t in range(2):
+                multiply(y_bank[h][u][:, t, :], ROW_TILE[h], bb_record(u, h), t * P, z_rec[q])
+
+        def add(q, u, h):
+            nc.vector.tensor_tensor(
+                out=y_sum[q][u][:, :, block(h)], in0=y_bank[h][u][:], in1=wx[q][u][:, :, block(h)], op=ADD
+            )
+
+        def sigmoid_of_sum(q, u):
+            nc.scalar.activation(out=result[q][u][:], in_=y_sum[q][u][:], func=SIGMOID)
+
+        def y_product(q, u, h):
+            rows = ROW_TILE[h]
+            for t in range(2):
+                dst = y_bank[h][u][:, t, :]
+                multiply(dst, rows, w_own[u], t * P, x_own[q][:, h], stop=False)
+                multiply(dst, rows, w_far[u], t * P, x_far[q], start=False, stop=False)
+                multiply(dst, rows, bb_record(u, h), t * P, z_rec[q], start=False)
+
+        def sigmoid_of_bank(q, u, h):
+            nc.scalar.activation(out=result[q][u][:, :, block(h)], in_=y_bank[h][u][:], func=SIGMOID)
+
+        def store(q, u):
+            dst = out[u * WIDE : (u + 1) * WIDE, q * WIDE : (q + 1) * WIDE]
+            nc.sync.dma_start(out=dst.rearrange("(t p) n -> p t n", p=P), in_=result[q][u][:])
+
+        vector, scalar, sync = nc.vector, nc.scalar, nc.sync
+
+        vector.memset(warm_up[:, 0:8], 0.0)
+        vector.memset(bb_own[:, WIDE:], 0)
+        for u in range(2):
+            vector.memset(w_own[u][:, WIDE:], 0)
+        for q in (2, 3):
+            vector.memset(x_own[q][:, :, P:], 0)
+        vector.memset(a_codes[:], 0)
+        vector.memset(a_scales[:].bitcast(I32), 0)
+
+        load(scalar, bb_raw[ROW_TILE[1]], bb[:, WIDE:M])
+        load(sync, bb_raw[ROW_TILE[0]], bb[:, 0:WIDE])
+        load(sync, a_raw[:], a)
+        load(sync, x_early[:], x[:, 0 : 2 * WIDE])
+        for u in range(2):
+            load(sync, w_raw[u][:], w[:, u * WIDE : (u + 1) * WIDE])
+        for q in (2, 3):
+            load(sync, x_raw[q], x[:, q * WIDE : (q + 1) * WIDE])
+        scalar.activation(out=warm_up[:, 8:9], in_=warm_up[:, 0:1], func=SIGMOID)
+
+        interleave(vector, bb_bf[:, block(0), :], bb_raw[:, :, block(0)])
+        interleave(scalar, bb_bf[:, block(1), :], bb_raw[:, :, block(1)])
+        quantize(bb_own, WIDE, bb_bf[:])
+        round_a(0)
+        round_a(1)
+        quantize_a(0)
+        quantize_a(1)
+        quantize_a(2)
+        quantize_a(3)
+
+        round_x(vector, 0, 0)
+        round_x(scalar, 0, 1)
+        round_x(vector, 1, 0)
+        round_x(scalar, 1, 1)
+        quantize_x(0, 0)
+        quantize_x(0, 1)
+        z_product(0)
+        quantize_x(1, 0)
+        quantize_x(1, 1)
+        z_product(1)
+
+        round_w(vector, 0, 0)
+        round_w(scalar, 0, 1)
+        bring_over(scalar, bb_far, bb_own, 0)
+        bring_over(scalar, bb_far, bb_own, 1)
+        quantize(w_own[0], WIDE, w_bf[0][:])
+        round_z(scalar, 0)
+
+        round_w(vector, 1, 0)
+        round_w(vector, 1, 1)
+        bring_over(sync, w_far[0], w_own[0], 0)
+        bring_over(sync, w_far[0], w_own[0], 1)
+        wx_product(0, 0)
+        wx_product(1, 0)
+        round_z(scalar, 1)
+        quantize_z(0)
+        quantize(w_own[1], WIDE, w_bf[1][:])
+        wx_copy(0, 0)
+        quantize_z(1)
+
+        lora_product(0, 0, 0)
+        lora_product(0, 1, 0)
+        bring_over(sync, w_far[1], w_own[1], 0)
+        bring_over(sync, w_far[1], w_own[1], 1)
+        round_x(vector, 2, 0)
+        round_x(vector, 2, 1)
+        wx_copy(1, 0)
+        wx_product(0, 1)
+        lora_product(0, 0, 1)
+        lora_product(0, 1, 1)
+        quantize_x(2, 0)
+        quantize_x(2, 1)
+        wx_copy(0, 1)
+        wx_product(1, 1)
+
+        add(0, 0, 0)
+        add(0, 0, 1)
+        bring_over(sync, x_far[2], x_own[2][:, 0], 0)
+        bring_over(sync, x_far[2], x_own[2][:, 1], 1)
+        z_product(2)
+        wx_copy(1, 1)
+        round_x(vector, 3, 0)
+        round_x(vector, 3, 1)
+        lora_product(1, 0, 0)
+        lora_product(1, 0, 1)
+        round_z(scalar, 2)
+        quantize_x(3, 0)
+        quantize_x(3, 1)
+
+        add(0, 1, 0)
+        add(0, 1, 1)
+        bring_over(sync, x_far[3], x_own[3][:, 0], 0)
+        bring_over(sync, x_far[3], x_own[3][:, 1], 1)
+        sigmoid_of_sum(0, 0)
+        z_product(3)
+        quantize_z(2)
+        sigmoid_of_sum(0, 1)
+        store(0, 0)
+        add(1, 0, 0)
+        lora_product(1, 1, 0)
+        add(1, 0, 1)
+
+        lora_product(1, 1, 1)
+        y_product(2, 0, 0)
+        add(1, 1, 0)
+        store(0, 1)
+        sigmoid_of_sum(1, 0)
+        round_z(vector, 3)
+        y_product(2, 0, 1)
+        sigmoid_of_bank(2, 0, 0)
+        store(1, 0)
+        add(1, 1, 1)
+        y_product(2, 1, 0)
+        sigmoid_of_bank(2, 0, 1)
+        quantize_z(3)
+        y_product(2, 1, 1)
+        sigmoid_of_sum(1, 1)
+        store(2, 0)
+
+        y_product(3, 0, 0)
+        sigmoid_of_bank(2, 1, 0)
+        store(1, 1)
+        sigmoid_of_bank(2, 1, 1)
+        y_product(3, 0, 1)
+        store(2, 1)
+        sigmoid_of_bank(3, 0, 0)
+        y_product(3, 1, 0)
+        sigmoid_of_bank(3, 0, 1)
+        store(3, 0)
+        y_product(3, 1, 1)
+        sigmoid_of_bank(3, 1, 0)
+        sigmoid_of_bank(3, 1, 1)
+        store(3, 1)

from contextlib import ExitStack

import concourse.mybir as mybir

K, R, M, N = 512, 256, 512, 1024
FLOPS = 2 * N * (K * R + K * M + R * M)

F32 = mybir.dt.float32
BF16 = mybir.dt.bfloat16
I32 = mybir.dt.int32
U8 = mybir.dt.uint8
FP8X4 = mybir.dt.float8_e4m3fn_x4
SIGMOID = mybir.ActivationFunctionType.Sigmoid
ADD = mybir.AluOpType.add

P = 128
HALF = 64
PACK = 4
WIDE = 256
ALIGN = 64
ALL_ROWS = slice(0, P)
ROW_TILE = (slice(0, HALF), slice(HALF, P))


def record_words(columns):
    return columns + columns // PACK


def codes(record, rows, first, count):
    return record[rows, first : first + count].bitcast(FP8X4)


def scales(record, rows, first, count):
    columns = record.shape[-1] * PACK // (PACK + 1)
    return record[rows, columns + first // PACK : columns + (first + count) // PACK].bitcast(U8)


def block(i):
    return slice(i * P, (i + 1) * P)


def tile_rows_lora_sigmoid_kernel(tc, x, w, a, bb, out):
    nc = tc.nc
    with ExitStack() as ctx:
        sb = ctx.enter_context(tc.tile_pool(name="sb", bufs=1))
        ps = ctx.enter_context(tc.psum_pool(name="ps", bufs=1))
        ctx.enter_context(tc.manual_schedule())

        def tiles(name, count, shape, dtype):
            return [sb.tile(shape, dtype, name="%s%d" % (name, i), align_bytes=ALIGN) for i in range(count)]

        a_raw = sb.tile([P, PACK, R], F32, name="a_raw", align_bytes=ALIGN)
        bb_raw = sb.tile([P, PACK, WIDE], F32, name="bb_raw", align_bytes=ALIGN)
        w_raw = tiles("w_raw", 2, [P, PACK, WIDE], F32)
        x_early = sb.tile([P, PACK, 2 * WIDE], F32, name="x_early", align_bytes=ALIGN)
        x_late = tiles("x_late", 2, [P, PACK, WIDE], F32)
        x_raw = [x_early[:, :, 0:WIDE], x_early[:, :, WIDE : 2 * WIDE], x_late[0][:], x_late[1][:]]

        a_bf = sb.tile([P, PACK, HALF, PACK], BF16, name="a_bf", align_bytes=ALIGN)
        bb_bf = sb.tile([P, WIDE, PACK], BF16, name="bb_bf", align_bytes=ALIGN)
        w_bf = tiles("w_bf", 2, [P, WIDE, PACK], BF16)
        x_bf = tiles("x_bf", 4, [P, WIDE, PACK], BF16)
        z_bf = tiles("z_bf", 4, [P, P, PACK], BF16)

        a_codes = sb.tile([P, (2 * PACK + 1) * HALF], I32, name="a_codes", align_bytes=ALIGN)
        a_scales = sb.tile([P, (2 * PACK + 1) * HALF], U8, name="a_scales", align_bytes=ALIGN)
        bb_own = sb.tile([P, record_words(WIDE)], I32, name="bb_own", align_bytes=ALIGN)
        bb_far = sb.tile([P, record_words(WIDE)], I32, name="bb_far", align_bytes=ALIGN)
        w_own = tiles("w_own", 2, [P, record_words(WIDE)], I32)
        w_far = tiles("w_far", 2, [P, record_words(WIDE)], I32)
        x_own = tiles("x_own", 4, [P, 2, record_words(P)], I32)
        x_far = dict(zip((2, 3), tiles("x_far", 2, [P, record_words(P)], I32)))
        z_rec = tiles("z_rec", 4, [P, record_words(P)], I32)

        wx = [tiles("wx%d_" % q, 2, [P, 2, WIDE], F32) for q in range(2)]
        y_sum = [tiles("y_sum%d_" % q, 2, [P, 2, WIDE], F32) for q in range(2)]
        result = [tiles("result%d_" % q, 2, [P, 2, WIDE], F32) for q in range(4)]
        warm_up = sb.tile([P, 16], F32, name="warm_up", align_bytes=ALIGN)

        z_bank = [ps.tile([P, PACK, P], F32, name="z_bank%d" % i) for i in range(2)]
        wx_bank = [ps.tile([P, 2, WIDE], F32, name="wx_bank%d" % q) for q in range(2)]
        y_bank = [[ps.tile([P, 2, P], F32, name="y_bank%d%d" % (h, u)) for u in range(2)] for h in range(2)]

        def copy(engine, dst, src):
            if engine is nc.vector:
                nc.vector.tensor_copy(out=dst, in_=src)
            else:
                nc.scalar.copy(out=dst, in_=src)

        def interleave(engine, dst, src):
            copy(
                engine,
                dst.rearrange("p (c i) j -> p c j i", i=PACK),
                src.rearrange("p j (c i) -> p c j i", i=PACK),
            )

        def quantize(record, count, values):
            nc.vector.quantize_mx(
                out=codes(record, ALL_ROWS, 0, count),
                scales=scales(record, ALL_ROWS, 0, count),
                in_=values.rearrange("p c j -> p (c j)"),
            )

        def multiply(dst, rows, lhs, lhs_first, rhs, start=True, stop=True):
            nc.tensor.matmul_mx(
                out=dst,
                lhsT=codes(lhs, rows, lhs_first, P),
                lhsT_scale=scales(lhs, rows, lhs_first, P),
                rhs=codes(rhs, rows, 0, P),
                rhs_scale=scales(rhs, rows, 0, P),
                start=start,
                stop=stop,
            )

        def load(queue, dst, src):
            queue.dma_start(out=dst, in_=src.rearrange("(p j) c -> p j c", j=PACK))

        def bring_over(queue, far, own, h):
            queue.dma_start(out=far[ROW_TILE[h]], in_=own[ROW_TILE[1 - h]])

        def round_a(h):
            nc.vector.tensor_copy(
                out=a_bf[:, :, 32 * h : 32 * (h + 1), :].rearrange("p i c j -> p c j i"),
                in_=a_raw[:, :, block(h)].rearrange("p j (c i) -> p c j i", i=PACK),
            )

        def quantize_a(j):
            columns = slice(HALF + P * j, P + P * j)
            nc.vector.quantize_mx(
                out=a_codes[:, columns].bitcast(FP8X4),
                scales=a_scales[:, columns],
                in_=a_bf[:, j].rearrange("p c i -> p (c i)"),
            )

        def round_w(engine, u, t):
            interleave(engine, w_bf[u][:, block(t), :], w_raw[u][:, :, block(t)])

        def round_x(engine, q, h):
            interleave(engine, x_bf[q][:, block(h), :], x_raw[q][:, :, block(h)])

        def quantize_x(q, h):
            quantize(x_own[q][:, h], P, x_bf[q][:, block(h), :])

        def z_product(q):
            for j in range(PACK):
                for h in range(2):
                    columns = slice(P * j + HALF * (1 - h), P * (j + 1) + HALF * (1 - h))
                    nc.tensor.matmul_mx(
                        out=z_bank[q % 2][:, j, :],
                        lhsT=a_codes[:, columns].bitcast(FP8X4),
                        lhsT_scale=a_scales[:, columns],
                        rhs=codes(x_own[q][:, h], ALL_ROWS, 0, P),
                        rhs_scale=scales(x_own[q][:, h], ALL_ROWS, 0, P),
                        start=(h == 0),
                        stop=(h == 1),
                    )

        def round_z(engine, q):
            interleave(engine, z_bf[q][:], z_bank[q % 2][:])

        def quantize_z(q):
            quantize(z_rec[q], P, z_bf[q][:])

        def bb_record(u, h):
            return bb_own if u == h else bb_far

        def wx_product(q, u):
            for t in range(2):
                for h in range(2):
                    multiply(wx_bank[q][:, t, block(h)], ALL_ROWS, w_own[u], t * P, x_own[q][:, h])

        def wx_copy(q, u):
            nc.scalar.copy(out=wx[q][u][:], in_=wx_bank[q][:])

        def lora_product(q, u, h):
            for t in range(2):
                multiply(y_bank[h][u][:, t, :], ROW_TILE[h], bb_record(u, h), t * P, z_rec[q])

        def add(q, u, h):
            nc.vector.tensor_tensor(
                out=y_sum[q][u][:, :, block(h)], in0=y_bank[h][u][:], in1=wx[q][u][:, :, block(h)], op=ADD
            )

        def sigmoid_of_sum(q, u):
            nc.scalar.activation(out=result[q][u][:], in_=y_sum[q][u][:], func=SIGMOID)

        def y_product(q, u, h):
            rows = ROW_TILE[h]
            for t in range(2):
                dst = y_bank[h][u][:, t, :]
                multiply(dst, rows, w_own[u], t * P, x_own[q][:, h], stop=False)
                multiply(dst, rows, w_far[u], t * P, x_far[q], start=False, stop=False)
                multiply(dst, rows, bb_record(u, h), t * P, z_rec[q], start=False)

        def sigmoid_of_bank(q, u, h):
            nc.scalar.activation(out=result[q][u][:, :, block(h)], in_=y_bank[h][u][:], func=SIGMOID)

        def store(q, u):
            dst = out[u * WIDE : (u + 1) * WIDE, q * WIDE : (q + 1) * WIDE]
            nc.sync.dma_start(out=dst.rearrange("(t p) n -> p t n", p=P), in_=result[q][u][:])

        vector, scalar, sync = nc.vector, nc.scalar, nc.sync

        vector.memset(warm_up[:, 0:8], 0.0)
        vector.memset(bb_own[:, WIDE:], 0)
        for u in range(2):
            vector.memset(w_own[u][:, WIDE:], 0)
        for q in (2, 3):
            vector.memset(x_own[q][:, :, P:], 0)
        vector.memset(a_codes[:], 0)
        vector.memset(a_scales[:].bitcast(I32), 0)

        load(scalar, bb_raw[ROW_TILE[1]], bb[:, WIDE:M])
        load(sync, bb_raw[ROW_TILE[0]], bb[:, 0:WIDE])
        load(sync, a_raw[:], a)
        load(sync, x_early[:], x[:, 0 : 2 * WIDE])
        for u in range(2):
            load(sync, w_raw[u][:], w[:, u * WIDE : (u + 1) * WIDE])
        for q in (2, 3):
            load(sync, x_raw[q], x[:, q * WIDE : (q + 1) * WIDE])
        scalar.activation(out=warm_up[:, 8:9], in_=warm_up[:, 0:1], func=SIGMOID)

        interleave(vector, bb_bf[:, block(0), :], bb_raw[:, :, block(0)])
        interleave(scalar, bb_bf[:, block(1), :], bb_raw[:, :, block(1)])
        quantize(bb_own, WIDE, bb_bf[:])
        round_a(0)
        round_a(1)
        quantize_a(0)
        quantize_a(1)
        quantize_a(2)
        quantize_a(3)

        round_x(vector, 0, 0)
        round_x(scalar, 0, 1)
        round_x(vector, 1, 0)
        round_x(scalar, 1, 1)
        quantize_x(0, 0)
        quantize_x(0, 1)
        z_product(0)
        quantize_x(1, 0)
        quantize_x(1, 1)
        z_product(1)

        round_w(vector, 0, 0)
        round_w(scalar, 0, 1)
        bring_over(scalar, bb_far, bb_own, 0)
        bring_over(scalar, bb_far, bb_own, 1)
        quantize(w_own[0], WIDE, w_bf[0][:])
        round_z(scalar, 0)

        round_w(vector, 1, 0)
        round_w(vector, 1, 1)
        bring_over(sync, w_far[0], w_own[0], 0)
        bring_over(sync, w_far[0], w_own[0], 1)
        wx_product(0, 0)
        wx_product(1, 0)
        round_z(scalar, 1)
        quantize_z(0)
        quantize(w_own[1], WIDE, w_bf[1][:])
        wx_copy(0, 0)
        quantize_z(1)

        lora_product(0, 0, 0)
        lora_product(0, 1, 0)
        bring_over(sync, w_far[1], w_own[1], 0)
        bring_over(sync, w_far[1], w_own[1], 1)
        round_x(vector, 2, 0)
        round_x(vector, 2, 1)
        wx_copy(1, 0)
        wx_product(0, 1)
        lora_product(0, 0, 1)
        lora_product(0, 1, 1)
        quantize_x(2, 0)
        quantize_x(2, 1)
        wx_copy(0, 1)
        wx_product(1, 1)

        add(0, 0, 0)
        add(0, 0, 1)
        bring_over(sync, x_far[2], x_own[2][:, 0], 0)
        bring_over(sync, x_far[2], x_own[2][:, 1], 1)
        z_product(2)
        wx_copy(1, 1)
        round_x(vector, 3, 0)
        round_x(vector, 3, 1)
        lora_product(1, 0, 0)
        lora_product(1, 0, 1)
        round_z(scalar, 2)
        quantize_x(3, 0)
        quantize_x(3, 1)

        add(0, 1, 0)
        add(0, 1, 1)
        bring_over(sync, x_far[3], x_own[3][:, 0], 0)
        bring_over(sync, x_far[3], x_own[3][:, 1], 1)
        sigmoid_of_sum(0, 0)
        z_product(3)
        quantize_z(2)
        sigmoid_of_sum(0, 1)
        store(0, 0)
        add(1, 0, 0)
        lora_product(1, 1, 0)
        add(1, 0, 1)

        lora_product(1, 1, 1)
        y_product(2, 0, 0)
        add(1, 1, 0)
        store(0, 1)
        sigmoid_of_sum(1, 0)
        round_z(vector, 3)
        y_product(2, 0, 1)
        sigmoid_of_bank(2, 0, 0)
        store(1, 0)
        add(1, 1, 1)
        y_product(2, 1, 0)
        sigmoid_of_bank(2, 0, 1)
        quantize_z(3)
        y_product(2, 1, 1)
        sigmoid_of_sum(1, 1)
        store(2, 0)

        y_product(3, 0, 0)
        sigmoid_of_bank(2, 1, 0)
        store(1, 1)
        sigmoid_of_bank(2, 1, 1)
        y_product(3, 0, 1)
        store(2, 1)
        sigmoid_of_bank(3, 0, 0)
        y_product(3, 1, 0)
        sigmoid_of_bank(3, 0, 1)
        store(3, 0)
        y_product(3, 1, 1)
        sigmoid_of_bank(3, 1, 0)
        sigmoid_of_bank(3, 1, 1)
        store(3, 1)
